import numpy as np
import ml_dtypes


def mxq(x, axis, fmt="e4m3"):
    dtype, down = {"e4m3": (ml_dtypes.float8_e4m3fn, 7), "e5m2": (ml_dtypes.float8_e5m2, 14)}[fmt]
    v = np.moveaxis(np.asarray(x, np.float32).astype(ml_dtypes.bfloat16).astype(np.float64), axis, -1)
    blocks = v.reshape(v.shape[:-1] + (-1, 32))
    amax = np.abs(blocks).max(-1, keepdims=True)
    byte = np.maximum(np.where(amax > 0, np.frexp(amax)[1] - 1 + 127, 0) - down, 1)
    scale = np.exp2(byte - 127.0)
    codes = (blocks / scale).astype(np.float32).astype(dtype).astype(np.float64)
    return np.moveaxis((codes * scale).reshape(v.shape), -1, axis)


WIDE = False


def mx_kscale(k):
    if not WIDE:
        return np.ones(k)
    levels = np.array([10, -10, 5, -5, 0])
    if k % 512:
        return np.exp2(np.random.permutation(np.resize(levels, k // 32))).repeat(32)
    a = np.empty((k // 512, 16))
    for p in range(k // 512):
        a[p, :8] = np.random.permutation(np.resize(levels, 8))
        for g in range(8):
            far = levels[np.abs(levels - a[p, g]) >= 10]
            a[p, g + 8] = far[np.random.randint(len(far))]
    return np.exp2(a.ravel()).repeat(32)


BF16 = ml_dtypes.bfloat16


def bf(x):
    return np.asarray(x, np.float32).astype(BF16)


def f64(x):
    return np.asarray(x).astype(np.float64)


E2M1 = np.array([0.0, 0.5, 1.0, 1.5, 2.0, 3.0, 4.0, 6.0, -0.0, -0.5, -1.0, -1.5, -2.0, -3.0, -4.0, -6.0])


def pack_weight(w, fmt):
    k, n = w.shape
    w = f64(bf(w)).reshape(k // 32, 32, n)
    amax = np.abs(w).max(1)
    if fmt == "e4m3":
        byte = np.frexp(amax)[1] - 1 + 127 - 7
    else:
        mant, ex = np.frexp(amax / 6.0)
        byte = np.where(mant > 0.5, ex, ex - 1) + 127
    byte = np.clip(np.where(amax > 0, byte, 1), 1, 254)
    scaled = (w * np.exp2(127.0 - byte)[:, None, :]).reshape(k, n).astype(np.float32)
    by_word = np.ascontiguousarray(scaled.reshape(k // 512, 128, 4, n).transpose(0, 1, 3, 2))
    if fmt == "e4m3":
        words = by_word.astype(ml_dtypes.float8_e4m3fn).view(np.uint8)
    else:
        c = by_word.astype(ml_dtypes.float4_e2m1fn).view(np.uint8) & 0xF
        words = c[..., 0::2] | (c[..., 1::2] << 4)
    return np.ascontiguousarray(words), np.ascontiguousarray(byte.astype(np.uint8).reshape(k // 512, 16, n))


def unpack_weight(words, scales, fmt):
    g, p, n, _ = words.shape
    if fmt == "e4m3":
        vals = np.ascontiguousarray(words).view(ml_dtypes.float8_e4m3fn).astype(np.float64)
    else:
        nib = np.empty((g, p, n, 4), np.uint8)
        nib[..., 0::2] = words & 0xF
        nib[..., 1::2] = words >> 4
        vals = E2M1[nib]
    vals = vals * np.repeat(np.exp2(scales.astype(np.float64) - 127.0), 8, axis=1)[..., None]
    return vals.transpose(0, 1, 3, 2).reshape(g * 512, n)
def pack4(w):
    words, scales = pack_weight(w, "e2m1")
    return words.reshape(words.shape[0], 128, -1), scales


def unpack4(words, scales):
    return unpack_weight(words.reshape(words.shape[0], 128, -1, 2), scales, "e2m1")


H, T, F, N = 4, 1024, 512, 1024


def setup_inputs():
    s = mx_kscale(H * T).reshape(H, T, 1)
    c = mx_kscale(H * F).reshape(H, 1, F)
    z = bf(np.random.standard_normal((H, T, F)) / np.sqrt(T) / s)
    phi = bf(np.random.standard_normal((H, T, F)) * s * c)
    nxt = bf(np.random.standard_normal((H, T, F)) * s * c)
    disc = bf(np.random.uniform(0.6, 0.99, (H, T)))
    w = np.random.standard_normal((H * F, N)) / np.sqrt(F) / c.reshape(H * F, 1)
    w_words, w_scales = pack4(w)
    b = bf(0.5 * np.random.standard_normal((H, F)))
    return {"z": z, "phi": phi, "nxt": nxt, "disc": disc,
            "w_words": w_words, "w_scales": w_scales, "b": b}


def reference(z, phi, nxt, disc, w_words, w_scales, b):
    d = f64(phi) - f64(disc)[:, :, None] * f64(nxt)
    zq = mxq(f64(z), 1, "e4m3")
    dq = mxq(d, 1, "e4m3")
    a = zq.swapaxes(1, 2) @ dq
    w = unpack4(w_words, w_scales).reshape(H, F, N)
    aw = mxq(a, 2, "e4m3") @ w
    return f64(b)[:, :, None] - aw

@@ -1,0 +1,284 @@
+from contextlib import ExitStack
+
+import concourse.mybir as mybir
+from concourse.masks import make_identity
+
+H, T, F, N = 4, 1024, 512, 1024
+FLOPS = 2 * H * F * F * T + 2 * H * F * F * N
+
+F32 = mybir.dt.float32
+BF16 = mybir.dt.bfloat16
+U32 = mybir.dt.uint32
+I32 = mybir.dt.int32
+U8 = mybir.dt.uint8
+FP8X4 = mybir.dt.float8_e4m3fn_x4
+FP4X4 = mybir.dt.float4_e2m1fn_x4
+ACT = mybir.ActivationFunctionType
+ALU = mybir.AluOpType
+
+P = 128
+PACK = 4
+K_PASS = P * PACK
+G = T // K_PASS
+CHUNKS = H * G
+TILES = F // P
+HALF = 512
+HALVES = N // HALF
+
+
+def tile_lstd_head_residuals_s14_kernel(tc, z, phi, nxt, disc, w_words, w_scales, b, out):
+    nc = tc.nc
+    with ExitStack() as ctx:
+        raw = ctx.enter_context(tc.tile_pool(name="raw", bufs=CHUNKS))
+        stage = ctx.enter_context(tc.tile_pool(name="stage", bufs=2))
+        zstage = ctx.enter_context(tc.tile_pool(name="zstage", bufs=4))
+        codes = ctx.enter_context(tc.tile_pool(name="codes", bufs=4))
+        acodes = ctx.enter_context(tc.tile_pool(name="acodes", bufs=4))
+        results = ctx.enter_context(tc.tile_pool(name="results", bufs=8))
+        keep = ctx.enter_context(tc.tile_pool(name="keep", bufs=1))
+        psum_a = ctx.enter_context(tc.psum_pool(name="psum_a", bufs=3))
+        psum_o = ctx.enter_context(tc.psum_pool(name="psum_o", bufs=5))
+        ctx.enter_context(tc.manual_schedule())
+
+        rows = keep.tile([P, F], BF16, name="rows")
+        w_sb = keep.tile([P, H, 2 * N], U8, name="w_sb", align_bytes=64)
+        ws_sb = keep.tile([P, H, N], U8, name="ws_sb", align_bytes=64)
+        ident = keep.tile([P, P], BF16, name="ident")
+        neg_disc = keep.tile([P, PACK, CHUNKS], F32, name="neg_disc")
+        b_cols = keep.tile([P, TILES, H], F32, name="b_cols")
+        warm = keep.tile([P, 2], F32, name="warm")
+
+        nc.vector.memset(rows[:], 0.0)
+        nc.vector.memset(warm[:], 0.0)
+        nc.vector.memset(ws_sb[:].rearrange("p g n -> p (g n)").bitcast(I32), 0)
+        make_identity(nc, ident[:])
+        nc.scalar.activation(out=warm[:, 1:2], in_=warm[:, 0:1], func=ACT.Identity)
+
+        z_raw, p_raw, n_raw = [], [], []
+
+        def load(lst, src, c, name, split=1):
+            h, g = divmod(c, G)
+            t = raw.tile([P, PACK, F], BF16, name=name)
+            view = src[h, g * K_PASS : (g + 1) * K_PASS, :].rearrange("(p j) w -> p j w", j=PACK)
+            lst.append(t)
+            return t, view
+
+        def load_whole(lst, src, c, name):
+            t, view = load(lst, src, c, name)
+            nc.sync.dma_start(out=t[:], in_=view)
+
+        load_whole(z_raw, z, 0, "z_raw")
+        nc.sync.dma_start(out=rows[0:CHUNKS, :], in_=disc.rearrange("h (g x) -> (h g) x", g=G))
+        nc.sync.dma_start(out=rows[CHUNKS : CHUNKS + H, :], in_=b)
+        nt, nv = load(n_raw, nxt, 0, "n_raw")
+        pt, pv = load(p_raw, phi, 0, "p_raw")
+        for j in (0, 2):
+            nc.sync.dma_start(out=nt[:, j : j + 2, :], in_=nv[:, j : j + 2, :])
+            nc.sync.dma_start(out=pt[:, j : j + 2, :], in_=pv[:, j : j + 2, :])
+        for c in range(1, 3):
+            load_whole(z_raw, z, c, "z_raw")
+            load_whole(n_raw, nxt, c, "n_raw")
+            load_whole(p_raw, phi, c, "p_raw")
+        load_whole(z_raw, z, 3, "z_raw")
+        for r in range(4):
+            nc.sync.dma_start(
+                out=ws_sb[r:P:32, :, :].bitcast(I32),
+                in_=w_scales[:, r:16:4, :].rearrange("g q n -> q g n").bitcast(I32),
+            )
+        nc.sync.dma_start(out=w_sb[:].bitcast(I32), in_=w_words.rearrange("g p x -> p g x").bitcast(I32))
+        load_whole(n_raw, nxt, 3, "n_raw")
+        load_whole(p_raw, phi, 3, "p_raw")
+        for c in range(4, CHUNKS):
+            load_whole(z_raw, z, c, "z_raw")
+            load_whole(n_raw, nxt, c, "n_raw")
+            load_whole(p_raw, phi, c, "p_raw")
+
+        turned = psum_a.tile([P, 2 * PACK, P], BF16, name="bank_a")
+        for j in range(PACK):
+            nc.tensor.transpose(turned[:, j, :], rows[:, j : F : PACK], ident[:])
+        for i in range(TILES):
+            nc.tensor.transpose(turned[:, PACK + i, :], rows[:, i * P : (i + 1) * P], ident[:])
+        nc.vector.tensor_scalar(
+            out=neg_disc[:], in0=turned[:, 0:PACK, 0:CHUNKS], scalar1=-1.0, scalar2=None, op0=ALU.mult
+        )
+        nc.vector.tensor_copy(out=b_cols[:], in_=turned[:, PACK : 2 * PACK, CHUNKS : CHUNKS + H])
+
+        z_grp, d_perm, d_grp = {}, {}, {}
+        z_codes, z_scales, d_codes, d_scales = {}, {}, {}, {}
+        bank_a, bank_o, a_grp, a_codes, a_scales, result = {}, {}, {}, {}, {}, {}
+
+        def interleave(engine_copy, dst, src, lo, hi):
+            engine_copy(
+                out=dst[:, lo:hi, :].rearrange("p (c i) t -> p c t i", i=4),
+                in_=src[:, :, lo:hi].rearrange("p t (c i) -> p c t i", i=4),
+            )
+
+        def new_z(c):
+            z_grp[c] = zstage.tile([P, F, PACK], BF16, name="z_grp", align_bytes=64)
+
+        def inter_z(c):
+            new_z(c)
+            interleave(nc.scalar.copy, z_grp[c], z_raw[c], 0, F)
+
+        def diff(c, j):
+            if j == 0:
+                d_perm[c] = stage.tile([P, PACK, F], BF16, name="d_perm")
+            nc.vector.scalar_tensor_tensor(
+                out=d_perm[c][:, j, :].rearrange("p (t m) -> p t m", t=PACK),
+                in0=n_raw[c][:, j, :].rearrange("p (m t) -> p t m", t=PACK),
+                scalar=neg_disc[:, j, c : c + 1],
+                in1=p_raw[c][:, j, :].rearrange("p (m t) -> p t m", t=PACK),
+                op0=ALU.mult,
+                op1=ALU.add,
+            )
+
+        def inter_d(c):
+            d_grp[c] = stage.tile([P, F, PACK], BF16, name="d_grp", align_bytes=64)
+            interleave(nc.vector.tensor_copy, d_grp[c], d_perm[c], 0, F)
+
+        def quant(c, grp, cd, sc, kind):
+            cd[c] = codes.tile([P, F], U32, name=kind + "_codes", align_bytes=64)
+            sc[c] = codes.tile([P, F], U8, name=kind + "_scales", align_bytes=64)
+            nc.vector.quantize_mx(
+                out=cd[c][:].bitcast(FP8X4), scales=sc[c][:], in_=grp[c][:].rearrange("p w t -> p (w t)")
+            )
+
+        def quant_z(c):
+            quant(c, z_grp, z_codes, z_scales, "z")
+
+        def quant_d(c):
+            quant(c, d_grp, d_codes, d_scales, "d")
+
+        def first_product(h, i):
+            bank = psum_a.tile([P, PACK, P], F32, name="bank_a")
+            bank_a[h, i] = bank
+            cols = slice(i * P, (i + 1) * P)
+            for t in range(PACK):
+                m = slice(t * P, (t + 1) * P)
+                for g in range(G):
+                    c = h * G + g
+                    nc.tensor.matmul_mx(
+                        out=bank[:, t, :],
+                        lhsT=d_codes[c][:, m].bitcast(FP8X4),
+                        lhsT_scale=d_scales[c][:, m],
+                        rhs=z_codes[c][:, cols].bitcast(FP8X4),
+                        rhs_scale=z_scales[c][:, cols],
+                        start=(g == 0),
+                        stop=(g == G - 1),
+                    )
+
+        def empty_a(copy, h, i):
+            a_grp[h, i] = acodes.tile([P, P, PACK], BF16, name="a_grp", align_bytes=64)
+            copy(out=a_grp[h, i][:], in_=bank_a[h, i][:].rearrange("p t n -> p n t"))
+
+        def quant_a(h, i):
+            a_codes[h, i] = acodes.tile([P, P], U32, name="a_codes", align_bytes=64)
+            a_scales[h, i] = acodes.tile([P, P], U8, name="a_scales", align_bytes=64)
+            nc.vector.quantize_mx(
+                out=a_codes[h, i][:].bitcast(FP8X4),
+                scales=a_scales[h, i][:],
+                in_=a_grp[h, i][:].rearrange("p n t -> p (n t)"),
+            )
+
+        def second_product(h, i):
+            for s in range(HALVES):
+                bank = psum_o.tile([P, HALF], F32, name="bank_o")
+                bank_o[h, i, s] = bank
+                nc.tensor.matmul_mx(
+                    out=bank[:],
+                    lhsT=a_codes[h, i][:].bitcast(FP8X4),
+                    lhsT_scale=a_scales[h, i][:],
+                    rhs=w_sb[:, h, 2 * HALF * s : 2 * HALF * (s + 1)].bitcast(FP4X4),
+                    rhs_scale=ws_sb[:, h, HALF * s : HALF * (s + 1)],
+                    start=True,
+                    stop=True,
+                )
+
+        def empty_o(on_vector, h, i, s):
+            if (h, i) not in result:
+                result[h, i] = results.tile([P, N], F32, name="result")
+            dst = result[h, i][:, HALF * s : HALF * (s + 1)]
+            bias = b_cols[:, i, h : h + 1]
+            if on_vector:
+                nc.vector.tensor_scalar(
+                    out=dst, in0=bank_o[h, i, s][:], scalar1=-1.0, scalar2=bias, op0=ALU.mult, op1=ALU.add
+                )
+            else:
+                nc.scalar.activation(out=dst, in_=bank_o[h, i, s][:], func=ACT.Identity, bias=bias, scale=-1.0)
+
+        def store(h, i, lo=0, hi=N):
+            nc.sync.dma_start(out=out[h, i * P : (i + 1) * P, lo:hi], in_=result[h, i][:, lo:hi])
+
+        s_copy, v_copy = nc.scalar.copy, nc.vector.tensor_copy
+
+        new_z(0)
+        interleave(nc.vector.tensor_copy, z_grp[0], z_raw[0], F // 2, F)
+        interleave(nc.scalar.copy, z_grp[0], z_raw[0], 0, F // 2)
+        for c in range(CHUNKS):
+            h = c // G - 1
+            first = c % G == 0
+            diff(c, 0)
+            if c > 0:
+                quant_d(c - 1)
+            if c == 0:
+                inter_z(1)
+                inter_z(2)
+            if c == 1:
+                inter_z(3)
+            if h >= 0 and first:
+                for i in range(TILES):
+                    first_product(h, i)
+                    empty_a(s_copy, h, i)
+            if h >= 0 and not first:
+                quant_a(h, 2)
+                second_product(h, 2)
+            diff(c, 1)
+            if h >= 0 and not first:
+                quant_a(h, 3)
+                second_product(h, 3)
+            diff(c, 2)
+            diff(c, 3)
+            quant_z(c)
+            if h >= 0 and first:
+                quant_a(h, 0)
+                second_product(h, 0)
+                empty_o(False, h, 0, 0)
+                empty_o(False, h, 0, 1)
+                store(h, 0)
+            inter_d(c)
+            if h >= 0 and first:
+                quant_a(h, 1)
+                second_product(h, 1)
+            if h >= 0 and not first:
+                for i in range(1, TILES):
+                    empty_o(False, h, i, 0)
+                    empty_o(False, h, i, 1)
+                    store(h, i)
+            if c >= 2 and c + 2 < CHUNKS:
+                inter_z(c + 2)
+
+        h = H - 1
+        quant_d(CHUNKS - 1)
+        first_product(h, 0)
+        empty_a(s_copy, h, 0)
+        first_product(h, 1)
+        quant_a(h, 0)
+        empty_a(v_copy, h, 1)
+        first_product(h, 2)
+        empty_a(s_copy, h, 2)
+        first_product(h, 3)
+        second_product(h, 0)
+        quant_a(h, 1)
+        second_product(h, 1)
+        empty_a(v_copy, h, 3)
+        quant_a(h, 2)
+        second_product(h, 2)
+        for s in range(HALVES):
+            empty_o(s == 1, h, 0, s)
+            store(h, 0, s * HALF, (s + 1) * HALF)
+        quant_a(h, 3)
+        second_product(h, 3)
+        for i in range(1, TILES):
+            for s in range(HALVES):
+                empty_o(s == 1, h, i, s)
+                store(h, i, s * HALF, (s + 1) * HALF)

@@ -36,8 +36,8 @@ def tile_lstd_head_residuals_s14_kernel(tc, z, phi, nxt, disc, w_words, w_scales
         acodes = ctx.enter_context(tc.tile_pool(name="acodes", bufs=4))
         results = ctx.enter_context(tc.tile_pool(name="results", bufs=8))
         keep = ctx.enter_context(tc.tile_pool(name="keep", bufs=1))
-        psum_a = ctx.enter_context(tc.psum_pool(name="psum_a", bufs=3))
-        psum_o = ctx.enter_context(tc.psum_pool(name="psum_o", bufs=5))
+        psum_a = ctx.enter_context(tc.psum_pool(name="psum_a", bufs=4))
+        psum_o = ctx.enter_context(tc.psum_pool(name="psum_o", bufs=4))
         ctx.enter_context(tc.manual_schedule())
 
         rows = keep.tile([P, F], BF16, name="rows")
@@ -52,7 +52,6 @@ def tile_lstd_head_residuals_s14_kernel(tc, z, phi, nxt, disc, w_words, w_scales
         nc.vector.memset(warm[:], 0.0)
         nc.vector.memset(ws_sb[:].rearrange("p g n -> p (g n)").bitcast(I32), 0)
         make_identity(nc, ident[:])
-        nc.scalar.activation(out=warm[:, 1:2], in_=warm[:, 0:1], func=ACT.Identity)
 
         z_raw, p_raw, n_raw = [], [], []
 
@@ -67,41 +66,46 @@ def tile_lstd_head_residuals_s14_kernel(tc, z, phi, nxt, disc, w_words, w_scales
             t, view = load(lst, src, c, name)
             nc.sync.dma_start(out=t[:], in_=view)
 
+        nc.scalar.dma_start(out=rows[0:CHUNKS, :], in_=disc.rearrange("h (g x) -> (h g) x", g=G))
+        nc.scalar.dma_start(out=rows[CHUNKS : CHUNKS + H, :], in_=b)
         load_whole(z_raw, z, 0, "z_raw")
-        nc.sync.dma_start(out=rows[0:CHUNKS, :], in_=disc.rearrange("h (g x) -> (h g) x", g=G))
-        nc.sync.dma_start(out=rows[CHUNKS : CHUNKS + H, :], in_=b)
+        nc.scalar.activation(out=warm[:, 1:2], in_=warm[:, 0:1], func=ACT.Identity)
         nt, nv = load(n_raw, nxt, 0, "n_raw")
         pt, pv = load(p_raw, phi, 0, "p_raw")
         for j in (0, 2):
             nc.sync.dma_start(out=nt[:, j : j + 2, :], in_=nv[:, j : j + 2, :])
             nc.sync.dma_start(out=pt[:, j : j + 2, :], in_=pv[:, j : j + 2, :])
-        for c in range(1, 3):
-            load_whole(z_raw, z, c, "z_raw")
+        def load_d(c):
             load_whole(n_raw, nxt, c, "n_raw")
             load_whole(p_raw, phi, c, "p_raw")
+
+        def load_w(h):
+            nc.sync.dma_start(out=w_sb[:, h, :].bitcast(I32), in_=w_words[h].bitcast(I32))
+
+        load_whole(z_raw, z, 1, "z_raw")
+        load_d(1)
+        load_whole(z_raw, z, 2, "z_raw")
+        load_d(2)
         load_whole(z_raw, z, 3, "z_raw")
         for r in range(4):
             nc.sync.dma_start(
                 out=ws_sb[r:P:32, :, :].bitcast(I32),
                 in_=w_scales[:, r:16:4, :].rearrange("g q n -> q g n").bitcast(I32),
             )
-        nc.sync.dma_start(out=w_sb[:].bitcast(I32), in_=w_words.rearrange("g p x -> p g x").bitcast(I32))
-        load_whole(n_raw, nxt, 3, "n_raw")
-        load_whole(p_raw, phi, 3, "p_raw")
+        load_w(0)
+        load_d(3)
         for c in range(4, CHUNKS):
             load_whole(z_raw, z, c, "z_raw")
-            load_whole(n_raw, nxt, c, "n_raw")
-            load_whole(p_raw, phi, c, "p_raw")
+            load_d(c)
+            if c % G == 0:
+                load_w(c // G - 1)
+        load_w(H - 1)
 
         turned = psum_a.tile([P, 2 * PACK, P], BF16, name="bank_a")
         for j in range(PACK):
             nc.tensor.transpose(turned[:, j, :], rows[:, j : F : PACK], ident[:])
         for i in range(TILES):
             nc.tensor.transpose(turned[:, PACK + i, :], rows[:, i * P : (i + 1) * P], ident[:])
-        nc.vector.tensor_scalar(
-            out=neg_disc[:], in0=turned[:, 0:PACK, 0:CHUNKS], scalar1=-1.0, scalar2=None, op0=ALU.mult
-        )
-        nc.vector.tensor_copy(out=b_cols[:], in_=turned[:, PACK : 2 * PACK, CHUNKS : CHUNKS + H])
 
         z_grp, d_perm, d_grp = {}, {}, {}
         z_codes, z_scales, d_codes, d_scales = {}, {}, {}, {}
@@ -120,40 +124,46 @@ def tile_lstd_head_residuals_s14_kernel(tc, z, phi, nxt, disc, w_words, w_scales
             new_z(c)
             interleave(nc.scalar.copy, z_grp[c], z_raw[c], 0, F)
 
-        def diff(c, j):
-            if j == 0:
+        def diff(c, j, ts=(0, PACK)):
+            if c not in d_perm:
                 d_perm[c] = stage.tile([P, PACK, F], BF16, name="d_perm")
+            t = slice(ts[0], ts[1])
             nc.vector.scalar_tensor_tensor(
-                out=d_perm[c][:, j, :].rearrange("p (t m) -> p t m", t=PACK),
-                in0=n_raw[c][:, j, :].rearrange("p (m t) -> p t m", t=PACK),
+                out=d_perm[c][:, j, :].rearrange("p (t m) -> p t m", t=PACK)[:, t, :],
+                in0=n_raw[c][:, j, :].rearrange("p (m t) -> p t m", t=PACK)[:, t, :],
                 scalar=neg_disc[:, j, c : c + 1],
-                in1=p_raw[c][:, j, :].rearrange("p (m t) -> p t m", t=PACK),
+                in1=p_raw[c][:, j, :].rearrange("p (m t) -> p t m", t=PACK)[:, t, :],
                 op0=ALU.mult,
                 op1=ALU.add,
             )
 
-        def inter_d(c):
-            d_grp[c] = stage.tile([P, F, PACK], BF16, name="d_grp", align_bytes=64)
-            interleave(nc.vector.tensor_copy, d_grp[c], d_perm[c], 0, F)
+        def inter_d(c, ts=(0, PACK), copy=nc.vector.tensor_copy):
+            if c not in d_grp:
+                d_grp[c] = stage.tile([P, F, PACK], BF16, name="d_grp", align_bytes=64)
+            interleave(copy, d_grp[c], d_perm[c], ts[0] * P, ts[1] * P)
 
-        def quant(c, grp, cd, sc, kind):
-            cd[c] = codes.tile([P, F], U32, name=kind + "_codes", align_bytes=64)
-            sc[c] = codes.tile([P, F], U8, name=kind + "_scales", align_bytes=64)
+        def quant(c, grp, cd, sc, kind, lo, hi):
+            if c not in cd:
+                cd[c] = codes.tile([P, F], U32, name=kind + "_codes", align_bytes=64)
+                sc[c] = codes.tile([P, F], U8, name=kind + "_scales", align_bytes=64)
             nc.vector.quantize_mx(
-                out=cd[c][:].bitcast(FP8X4), scales=sc[c][:], in_=grp[c][:].rearrange("p w t -> p (w t)")
+                out=cd[c][:, lo:hi].bitcast(FP8X4),
+                scales=sc[c][:, lo:hi],
+                in_=grp[c][:, lo:hi, :].rearrange("p w t -> p (w t)"),
             )
 
         def quant_z(c):
-            quant(c, z_grp, z_codes, z_scales, "z")
+            quant(c, z_grp, z_codes, z_scales, "z", 0, F)
 
-        def quant_d(c):
-            quant(c, d_grp, d_codes, d_scales, "d")
+        def quant_d(c, ts=(0, PACK)):
+            quant(c, d_grp, d_codes, d_scales, "d", ts[0] * P, ts[1] * P)
 
-        def first_product(h, i):
-            bank = psum_a.tile([P, PACK, P], F32, name="bank_a")
-            bank_a[h, i] = bank
+        def first_product(h, i, ts=(0, PACK)):
+            if (h, i) not in bank_a:
+                bank_a[h, i] = psum_a.tile([P, PACK, P], F32, name="bank_a")
+            bank = bank_a[h, i]
             cols = slice(i * P, (i + 1) * P)
-            for t in range(PACK):
+            for t in range(ts[0], ts[1]):
                 m = slice(t * P, (t + 1) * P)
                 for g in range(G):
                     c = h * G + g
@@ -211,74 +221,77 @@ def tile_lstd_head_residuals_s14_kernel(tc, z, phi, nxt, disc, w_words, w_scales
 
         s_copy, v_copy = nc.scalar.copy, nc.vector.tensor_copy
 
-        new_z(0)
-        interleave(nc.vector.tensor_copy, z_grp[0], z_raw[0], F // 2, F)
-        interleave(nc.scalar.copy, z_grp[0], z_raw[0], 0, F // 2)
+        nc.vector.tensor_scalar(
+            out=neg_disc[:], in0=turned[:, 0:PACK, 0:CHUNKS], scalar1=-1.0, scalar2=None, op0=ALU.mult
+        )
+        inter_z(0)
+        inter_z(1)
+        inter_z(2)
+        inter_z(3)
+        last = CHUNKS - 1
+        ZPOS = 2
+        V_O = ((), (), ())
+        lo, hi = (0, PACK // 2), (PACK // 2, PACK)
         for c in range(CHUNKS):
             h = c // G - 1
             first = c % G == 0
-            diff(c, 0)
-            if c > 0:
-                quant_d(c - 1)
-            if c == 0:
-                inter_z(1)
-                inter_z(2)
-            if c == 1:
-                inter_z(3)
-            if h >= 0 and first:
-                for i in range(TILES):
-                    first_product(h, i)
-                    empty_a(s_copy, h, i)
-            if h >= 0 and not first:
-                quant_a(h, 2)
-                second_product(h, 2)
-            diff(c, 1)
-            if h >= 0 and not first:
-                quant_a(h, 3)
-                second_product(h, 3)
-            diff(c, 2)
-            diff(c, 3)
+            parts = (lo, hi) if c == last else ((0, PACK),)
+            late = (h >= 0 and not first)
+            for q in range(PACK):
+                diff(c, q, parts[0])
+                if q == 0 and c > 0:
+                    quant_d(c - 1)
+                    if first and h >= 0:
+                        for i in range(TILES):
+                            first_product(h, i)
+                            empty_a(s_copy, h, i)
+                if q == 1 and c == 1:
+                    nc.vector.tensor_copy(out=b_cols[:], in_=turned[:, PACK : 2 * PACK, CHUNKS : CHUNKS + H])
+                if late:
+                    quant_a(h, q)
+                    second_product(h, q)
             quant_z(c)
-            if h >= 0 and first:
-                quant_a(h, 0)
-                second_product(h, 0)
-                empty_o(False, h, 0, 0)
-                empty_o(False, h, 0, 1)
-                store(h, 0)
-            inter_d(c)
-            if h >= 0 and first:
-                quant_a(h, 1)
-                second_product(h, 1)
-            if h >= 0 and not first:
-                for i in range(1, TILES):
-                    empty_o(False, h, i, 0)
-                    empty_o(False, h, i, 1)
-                    store(h, i)
-            if c >= 2 and c + 2 < CHUNKS:
+            if late:
+                for i, s in V_O[h]:
+                    empty_o(True, h, i, s)
+            inter_d(c, parts[0])
+            if c == last:
+                diff(c, 0, hi)
+                quant_d(c, lo)
+                for i in range(TILES):
+                    first_product(H - 1, i, lo)
+                for q in (1, 2, 3):
+                    diff(c, q, hi)
+                inter_d(c, hi)
+            if h >= 0 and first and c + 2 < CHUNKS:
                 inter_z(c + 2)
+            if late:
+                for i in range(TILES):
+                    if i == ZPOS and c + 2 < CHUNKS:
+                        inter_z(c + 2)
+                    for s in range(HALVES):
+                        if (i, s) not in V_O[h]:
+                            empty_o(False, h, i, s)
+                    store(h, i)
 
         h = H - 1
-        quant_d(CHUNKS - 1)
-        first_product(h, 0)
+        quant_d(last, hi)
+        for i in range(TILES):
+            first_product(h, i, hi)
         empty_a(s_copy, h, 0)
-        first_product(h, 1)
-        quant_a(h, 0)
         empty_a(v_copy, h, 1)
-        first_product(h, 2)
         empty_a(s_copy, h, 2)
-        first_product(h, 3)
+        quant_a(h, 0)
         second_product(h, 0)
+        empty_a(v_copy, h, 3)
         quant_a(h, 1)
         second_product(h, 1)
-        empty_a(v_copy, h, 3)
         quant_a(h, 2)
         second_product(h, 2)
-        for s in range(HALVES):
-            empty_o(s == 1, h, 0, s)
-            store(h, 0, s * HALF, (s + 1) * HALF)
-        quant_a(h, 3)
-        second_product(h, 3)
-        for i in range(1, TILES):
+        for i in range(TILES):
             for s in range(HALVES):
                 empty_o(s == 1, h, i, s)
                 store(h, i, s * HALF, (s + 1) * HALF)
+            if i == 0:
+                quant_a(h, 3)
+                second_product(h, 3)

@@ -41,6 +41,7 @@ def tile_lstd_head_residuals_s14_kernel(tc, z, phi, nxt, disc, w_words, w_scales
         ctx.enter_context(tc.manual_schedule())
 
         rows = keep.tile([P, F], BF16, name="rows")
+        b_rows = keep.tile([P, F], BF16, name="b_rows")
         w_sb = keep.tile([P, H, 2 * N], U8, name="w_sb", align_bytes=64)
         ws_sb = keep.tile([P, H, N], U8, name="ws_sb", align_bytes=64)
         ident = keep.tile([P, P], BF16, name="ident")
@@ -48,8 +49,9 @@ def tile_lstd_head_residuals_s14_kernel(tc, z, phi, nxt, disc, w_words, w_scales
         b_cols = keep.tile([P, TILES, H], F32, name="b_cols")
         warm = keep.tile([P, 2], F32, name="warm")
 
-        nc.vector.memset(rows[:], 0.0)
+        nc.gpsimd.memset(rows[:].bitcast(I32), 0)
         nc.vector.memset(warm[:], 0.0)
+        nc.vector.memset(b_rows[:], 0.0)
         nc.vector.memset(ws_sb[:].rearrange("p g n -> p (g n)").bitcast(I32), 0)
         make_identity(nc, ident[:])
 
@@ -66,9 +68,8 @@ def tile_lstd_head_residuals_s14_kernel(tc, z, phi, nxt, disc, w_words, w_scales
             t, view = load(lst, src, c, name)
             nc.sync.dma_start(out=t[:], in_=view)
 
-        nc.scalar.dma_start(out=rows[0:CHUNKS, :], in_=disc.rearrange("h (g x) -> (h g) x", g=G))
-        nc.scalar.dma_start(out=rows[CHUNKS : CHUNKS + H, :], in_=b)
         load_whole(z_raw, z, 0, "z_raw")
+        nc.sync.dma_start(out=rows[0:CHUNKS, :], in_=disc.rearrange("h (g x) -> (h g) x", g=G))
         nc.scalar.activation(out=warm[:, 1:2], in_=warm[:, 0:1], func=ACT.Identity)
         nt, nv = load(n_raw, nxt, 0, "n_raw")
         pt, pv = load(p_raw, phi, 0, "p_raw")
@@ -83,6 +84,7 @@ def tile_lstd_head_residuals_s14_kernel(tc, z, phi, nxt, disc, w_words, w_scales
             nc.sync.dma_start(out=w_sb[:, h, :].bitcast(I32), in_=w_words[h].bitcast(I32))
 
         load_whole(z_raw, z, 1, "z_raw")
+        nc.sync.dma_start(out=b_rows[0:H, :], in_=b)
         load_d(1)
         load_whole(z_raw, z, 2, "z_raw")
         load_d(2)
@@ -101,11 +103,12 @@ def tile_lstd_head_residuals_s14_kernel(tc, z, phi, nxt, disc, w_words, w_scales
                 load_w(c // G - 1)
         load_w(H - 1)
 
-        turned = psum_a.tile([P, 2 * PACK, P], BF16, name="bank_a")
+        turned = psum_a.tile([P, PACK, P], BF16, name="bank_a")
         for j in range(PACK):
             nc.tensor.transpose(turned[:, j, :], rows[:, j : F : PACK], ident[:])
-        for i in range(TILES):
-            nc.tensor.transpose(turned[:, PACK + i, :], rows[:, i * P : (i + 1) * P], ident[:])
+        nc.vector.tensor_scalar(
+            out=neg_disc[:], in0=turned[:, :, 0:CHUNKS], scalar1=-1.0, scalar2=None, op0=ALU.mult
+        )
 
         z_grp, d_perm, d_grp = {}, {}, {}
         z_codes, z_scales, d_codes, d_scales = {}, {}, {}, {}
@@ -221,9 +224,6 @@ def tile_lstd_head_residuals_s14_kernel(tc, z, phi, nxt, disc, w_words, w_scales
 
         s_copy, v_copy = nc.scalar.copy, nc.vector.tensor_copy
 
-        nc.vector.tensor_scalar(
-            out=neg_disc[:], in0=turned[:, 0:PACK, 0:CHUNKS], scalar1=-1.0, scalar2=None, op0=ALU.mult
-        )
         inter_z(0)
         inter_z(1)
         inter_z(2)
@@ -246,7 +246,10 @@ def tile_lstd_head_residuals_s14_kernel(tc, z, phi, nxt, disc, w_words, w_scales
                             first_product(h, i)
                             empty_a(s_copy, h, i)
                 if q == 1 and c == 1:
-                    nc.vector.tensor_copy(out=b_cols[:], in_=turned[:, PACK : 2 * PACK, CHUNKS : CHUNKS + H])
+                    turned_b = psum_a.tile([P, TILES, P], BF16, name="bank_a")
+                    for i in range(TILES):
+                        nc.tensor.transpose(turned_b[:, i, :], b_rows[:, i * P : (i + 1) * P], ident[:])
+                    nc.vector.tensor_copy(out=b_cols[:], in_=turned_b[:, :, 0:H])
                 if late:
                     quant_a(h, q)
                     second_product(h, q)

@@ -73,9 +73,9 @@ def tile_lstd_head_residuals_s14_kernel(tc, z, phi, nxt, disc, w_words, w_scales
         nc.scalar.activation(out=warm[:, 1:2], in_=warm[:, 0:1], func=ACT.Identity)
         nt, nv = load(n_raw, nxt, 0, "n_raw")
         pt, pv = load(p_raw, phi, 0, "p_raw")
-        for j in (0, 2):
-            nc.sync.dma_start(out=nt[:, j : j + 2, :], in_=nv[:, j : j + 2, :])
-            nc.sync.dma_start(out=pt[:, j : j + 2, :], in_=pv[:, j : j + 2, :])
+        for j0, j1 in ((0, 1), (1, 2), (2, 4)):
+            nc.sync.dma_start(out=nt[:, j0:j1, :], in_=nv[:, j0:j1, :])
+            nc.sync.dma_start(out=pt[:, j0:j1, :], in_=pv[:, j0:j1, :])
         def load_d(c):
             load_whole(n_raw, nxt, c, "n_raw")
             load_whole(p_raw, phi, c, "p_raw")
@@ -83,19 +83,26 @@ def tile_lstd_head_residuals_s14_kernel(tc, z, phi, nxt, disc, w_words, w_scales
         def load_w(h):
             nc.sync.dma_start(out=w_sb[:, h, :].bitcast(I32), in_=w_words[h].bitcast(I32))
 
+        def load_d_halves(c):
+            nt, nv = load(n_raw, nxt, c, "n_raw")
+            pt, pv = load(p_raw, phi, c, "p_raw")
+            for j0, j1 in ((0, 2), (2, 4)):
+                nc.sync.dma_start(out=nt[:, j0:j1, :], in_=nv[:, j0:j1, :])
+                nc.sync.dma_start(out=pt[:, j0:j1, :], in_=pv[:, j0:j1, :])
+
         load_whole(z_raw, z, 1, "z_raw")
-        nc.sync.dma_start(out=b_rows[0:H, :], in_=b)
-        load_d(1)
+        load_d_halves(1)
         load_whole(z_raw, z, 2, "z_raw")
-        load_d(2)
+        nc.sync.dma_start(out=b_rows[0:H, :], in_=b)
         load_whole(z_raw, z, 3, "z_raw")
+        load_d_halves(2)
+        load_d(3)
         for r in range(4):
             nc.sync.dma_start(
                 out=ws_sb[r:P:32, :, :].bitcast(I32),
                 in_=w_scales[:, r:16:4, :].rearrange("g q n -> q g n").bitcast(I32),
             )
         load_w(0)
-        load_d(3)
         for c in range(4, CHUNKS):
             load_whole(z_raw, z, c, "z_raw")
             load_d(c)
@@ -181,16 +188,21 @@ def tile_lstd_head_residuals_s14_kernel(tc, z, phi, nxt, disc, w_words, w_scales
                     )
 
         def empty_a(copy, h, i):
-            a_grp[h, i] = acodes.tile([P, P, PACK], BF16, name="a_grp", align_bytes=64)
-            copy(out=a_grp[h, i][:], in_=bank_a[h, i][:].rearrange("p t n -> p n t"))
+            if i % 2 == 0:
+                a_grp[h, i // 2] = acodes.tile([P, 2 * P, PACK], BF16, name="a_grp", align_bytes=64)
+            n = slice(i % 2 * P, (i % 2 + 1) * P)
+            copy(out=a_grp[h, i // 2][:, n, :], in_=bank_a[h, i][:].rearrange("p t n -> p n t"))
 
-        def quant_a(h, i):
-            a_codes[h, i] = acodes.tile([P, P], U32, name="a_codes", align_bytes=64)
-            a_scales[h, i] = acodes.tile([P, P], U8, name="a_scales", align_bytes=64)
+        def quant_a(h, first_tile, tiles):
+            k = first_tile // 2
+            if (h, k) not in a_codes:
+                a_codes[h, k] = acodes.tile([P, 2 * P], U32, name="a_codes", align_bytes=64)
+                a_scales[h, k] = acodes.tile([P, 2 * P], U8, name="a_scales", align_bytes=64)
+            n = slice(first_tile % 2 * P, (first_tile % 2 + tiles) * P)
             nc.vector.quantize_mx(
-                out=a_codes[h, i][:].bitcast(FP8X4),
-                scales=a_scales[h, i][:],
-                in_=a_grp[h, i][:].rearrange("p n t -> p (n t)"),
+                out=a_codes[h, k][:, n].bitcast(FP8X4),
+                scales=a_scales[h, k][:, n],
+                in_=a_grp[h, k][:, n, :].rearrange("p n t -> p (n t)"),
             )
 
         def second_product(h, i):
@@ -199,8 +211,8 @@ def tile_lstd_head_residuals_s14_kernel(tc, z, phi, nxt, disc, w_words, w_scales
                 bank_o[h, i, s] = bank
                 nc.tensor.matmul_mx(
                     out=bank[:],
-                    lhsT=a_codes[h, i][:].bitcast(FP8X4),
-                    lhsT_scale=a_scales[h, i][:],
+                    lhsT=a_codes[h, i // 2][:, i % 2 * P : (i % 2 + 1) * P].bitcast(FP8X4),
+                    lhsT_scale=a_scales[h, i // 2][:, i % 2 * P : (i % 2 + 1) * P],
                     rhs=w_sb[:, h, 2 * HALF * s : 2 * HALF * (s + 1)].bitcast(FP4X4),
                     rhs_scale=ws_sb[:, h, HALF * s : HALF * (s + 1)],
                     start=True,
@@ -230,7 +242,7 @@ def tile_lstd_head_residuals_s14_kernel(tc, z, phi, nxt, disc, w_words, w_scales
         inter_z(3)
         last = CHUNKS - 1
         ZPOS = 2
-        V_O = ((), (), ())
+        V_O = (((0,1),), ((0,1),), ())
         lo, hi = (0, PACK // 2), (PACK // 2, PACK)
         for c in range(CHUNKS):
             h = c // G - 1
@@ -250,8 +262,9 @@ def tile_lstd_head_residuals_s14_kernel(tc, z, phi, nxt, disc, w_words, w_scales
                     for i in range(TILES):
                         nc.tensor.transpose(turned_b[:, i, :], b_rows[:, i * P : (i + 1) * P], ident[:])
                     nc.vector.tensor_copy(out=b_cols[:], in_=turned_b[:, :, 0:H])
-                if late:
-                    quant_a(h, q)
+                if late and q % 2 == 1:
+                    quant_a(h, q - 1, 2)
+                    second_product(h, q - 1)
                     second_product(h, q)
             quant_z(c)
             if late:
@@ -282,19 +295,19 @@ def tile_lstd_head_residuals_s14_kernel(tc, z, phi, nxt, disc, w_words, w_scales
         for i in range(TILES):
             first_product(h, i, hi)
         empty_a(s_copy, h, 0)
-        empty_a(v_copy, h, 1)
+        empty_a(s_copy, h, 1)
         empty_a(s_copy, h, 2)
-        quant_a(h, 0)
+        quant_a(h, 0, 1)
         second_product(h, 0)
         empty_a(v_copy, h, 3)
-        quant_a(h, 1)
+        quant_a(h, 1, 1)
         second_product(h, 1)
-        quant_a(h, 2)
+        quant_a(h, 2, 1)
         second_product(h, 2)
         for i in range(TILES):
             for s in range(HALVES):
                 empty_o(s == 1, h, i, s)
                 store(h, i, s * HALF, (s + 1) * HALF)
             if i == 0:
-                quant_a(h, 3)
+                quant_a(h, 3, 1)
                 second_product(h, 3)

@@ -29,12 +29,12 @@ HALVES = N // HALF
 def tile_lstd_head_residuals_s14_kernel(tc, z, phi, nxt, disc, w_words, w_scales, b, out):
     nc = tc.nc
     with ExitStack() as ctx:
-        raw = ctx.enter_context(tc.tile_pool(name="raw", bufs=CHUNKS))
+        raw = ctx.enter_context(tc.tile_pool(name="raw", bufs=H))
         stage = ctx.enter_context(tc.tile_pool(name="stage", bufs=2))
         zstage = ctx.enter_context(tc.tile_pool(name="zstage", bufs=4))
         codes = ctx.enter_context(tc.tile_pool(name="codes", bufs=4))
         acodes = ctx.enter_context(tc.tile_pool(name="acodes", bufs=4))
-        results = ctx.enter_context(tc.tile_pool(name="results", bufs=8))
+        results = ctx.enter_context(tc.tile_pool(name="results", bufs=4))
         keep = ctx.enter_context(tc.tile_pool(name="keep", bufs=1))
         psum_a = ctx.enter_context(tc.psum_pool(name="psum_a", bufs=4))
         psum_o = ctx.enter_context(tc.psum_pool(name="psum_o", bufs=4))
@@ -55,60 +55,56 @@ def tile_lstd_head_residuals_s14_kernel(tc, z, phi, nxt, disc, w_words, w_scales
         nc.vector.memset(ws_sb[:].rearrange("p g n -> p (g n)").bitcast(I32), 0)
         make_identity(nc, ident[:])
 
-        z_raw, p_raw, n_raw = [], [], []
+        z_raw, n_raw, p_raw = [], [], []
+        for h in range(H):
+            z_head = raw.tile([P, G, PACK, F], BF16, name="z_head")
+            n_head = raw.tile([P, G, PACK, F], BF16, name="n_head")
+            p_head = raw.tile([P, G, PACK, F], BF16, name="p_head")
+            z_raw.append(z_head)
+            n_raw.append(n_head)
+            p_raw.append(p_head)
 
-        def load(lst, src, c, name, split=1):
+        def load_rows(dst, src, c, j0=0, j1=PACK):
             h, g = divmod(c, G)
-            t = raw.tile([P, PACK, F], BF16, name=name)
             view = src[h, g * K_PASS : (g + 1) * K_PASS, :].rearrange("(p j) w -> p j w", j=PACK)
-            lst.append(t)
-            return t, view
+            nc.sync.dma_start(out=dst[h][:, g, j0:j1, :], in_=view[:, j0:j1, :])
 
-        def load_whole(lst, src, c, name):
-            t, view = load(lst, src, c, name)
-            nc.sync.dma_start(out=t[:], in_=view)
+        def load_head(dst, src, h):
+            nc.sync.dma_start(out=dst[h][:], in_=src[h].rearrange("(g p j) w -> p g j w", g=G, j=PACK))
 
-        load_whole(z_raw, z, 0, "z_raw")
-        nc.sync.dma_start(out=rows[0:CHUNKS, :], in_=disc.rearrange("h (g x) -> (h g) x", g=G))
         nc.scalar.activation(out=warm[:, 1:2], in_=warm[:, 0:1], func=ACT.Identity)
-        nt, nv = load(n_raw, nxt, 0, "n_raw")
-        pt, pv = load(p_raw, phi, 0, "p_raw")
-        for j0, j1 in ((0, 1), (1, 2), (2, 4)):
-            nc.sync.dma_start(out=nt[:, j0:j1, :], in_=nv[:, j0:j1, :])
-            nc.sync.dma_start(out=pt[:, j0:j1, :], in_=pv[:, j0:j1, :])
-        def load_d(c):
-            load_whole(n_raw, nxt, c, "n_raw")
-            load_whole(p_raw, phi, c, "p_raw")
-
-        def load_w(h):
-            nc.sync.dma_start(out=w_sb[:, h, :].bitcast(I32), in_=w_words[h].bitcast(I32))
-
-        def load_d_halves(c):
-            nt, nv = load(n_raw, nxt, c, "n_raw")
-            pt, pv = load(p_raw, phi, c, "p_raw")
-            for j0, j1 in ((0, 2), (2, 4)):
-                nc.sync.dma_start(out=nt[:, j0:j1, :], in_=nv[:, j0:j1, :])
-                nc.sync.dma_start(out=pt[:, j0:j1, :], in_=pv[:, j0:j1, :])
-
-        load_whole(z_raw, z, 1, "z_raw")
-        load_d_halves(1)
-        load_whole(z_raw, z, 2, "z_raw")
+        load_rows(z_raw, z, 0)
+        nc.sync.dma_start(out=rows[0:CHUNKS, :], in_=disc.rearrange("h (g x) -> (h g) x", g=G))
+        load_rows(n_raw, nxt, 0, 0, 2)
+        load_rows(p_raw, phi, 0, 0, 2)
+        load_rows(n_raw, nxt, 0, 2, 4)
+        load_rows(p_raw, phi, 0, 2, 4)
+        load_rows(z_raw, z, 1)
         nc.sync.dma_start(out=b_rows[0:H, :], in_=b)
-        load_whole(z_raw, z, 3, "z_raw")
-        load_d_halves(2)
-        load_d(3)
+        load_rows(n_raw, nxt, 1)
+        load_rows(p_raw, phi, 1)
+        load_rows(z_raw, z, 2)
+        load_rows(n_raw, nxt, 2)
+        load_rows(p_raw, phi, 2)
+        load_rows(z_raw, z, 3)
         for r in range(4):
             nc.sync.dma_start(
                 out=ws_sb[r:P:32, :, :].bitcast(I32),
                 in_=w_scales[:, r:16:4, :].rearrange("g q n -> q g n").bitcast(I32),
             )
-        load_w(0)
-        for c in range(4, CHUNKS):
-            load_whole(z_raw, z, c, "z_raw")
-            load_d(c)
-            if c % G == 0:
-                load_w(c // G - 1)
-        load_w(H - 1)
+        nc.sync.dma_start(out=w_sb[:, 0:1, :].bitcast(I32), in_=w_words[0:1].rearrange("g p x -> p g x").bitcast(I32))
+        load_rows(n_raw, nxt, 3)
+        load_rows(p_raw, phi, 3)
+        load_rows(z_raw, z, 4)
+        load_rows(n_raw, nxt, 4)
+        load_rows(p_raw, phi, 4)
+        load_rows(z_raw, z, 5)
+        load_rows(n_raw, nxt, 5)
+        load_rows(p_raw, phi, 5)
+        nc.sync.dma_start(out=w_sb[:, 1:4, :].bitcast(I32), in_=w_words[1:4].rearrange("g p x -> p g x").bitcast(I32))
+        load_head(z_raw, z, 3)
+        load_head(n_raw, nxt, 3)
+        load_head(p_raw, phi, 3)
 
         turned = psum_a.tile([P, PACK, P], BF16, name="bank_a")
         for j in range(PACK):
@@ -117,7 +113,7 @@ def tile_lstd_head_residuals_s14_kernel(tc, z, phi, nxt, disc, w_words, w_scales
             out=neg_disc[:], in0=turned[:, :, 0:CHUNKS], scalar1=-1.0, scalar2=None, op0=ALU.mult
         )
 
-        z_grp, d_perm, d_grp = {}, {}, {}
+        z_grp, d_perm, d_grp, scaled = {}, {}, {}, {}
         z_codes, z_scales, d_codes, d_scales = {}, {}, {}, {}
         bank_a, bank_o, a_grp, a_codes, a_scales, result = {}, {}, {}, {}, {}, {}
 
@@ -132,7 +128,7 @@ def tile_lstd_head_residuals_s14_kernel(tc, z, phi, nxt, disc, w_words, w_scales
 
         def inter_z(c):
             new_z(c)
-            interleave(nc.scalar.copy, z_grp[c], z_raw[c], 0, F)
+            interleave(nc.scalar.copy, z_grp[c], z_raw[c // G][:, c % G, :, :], 0, F)
 
         def diff(c, j, ts=(0, PACK)):
             if c not in d_perm:
@@ -140,9 +136,9 @@ def tile_lstd_head_residuals_s14_kernel(tc, z, phi, nxt, disc, w_words, w_scales
             t = slice(ts[0], ts[1])
             nc.vector.scalar_tensor_tensor(
                 out=d_perm[c][:, j, :].rearrange("p (t m) -> p t m", t=PACK)[:, t, :],
-                in0=n_raw[c][:, j, :].rearrange("p (m t) -> p t m", t=PACK)[:, t, :],
+                in0=n_raw[c // G][:, c % G, j, :].rearrange("p (m t) -> p t m", t=PACK)[:, t, :],
                 scalar=neg_disc[:, j, c : c + 1],
-                in1=p_raw[c][:, j, :].rearrange("p (m t) -> p t m", t=PACK)[:, t, :],
+                in1=p_raw[c // G][:, c % G, j, :].rearrange("p (m t) -> p t m", t=PACK)[:, t, :],
                 op0=ALU.mult,
                 op1=ALU.add,
             )
@@ -151,6 +147,32 @@ def tile_lstd_head_residuals_s14_kernel(tc, z, phi, nxt, disc, w_words, w_scales
             if c not in d_grp:
                 d_grp[c] = stage.tile([P, F, PACK], BF16, name="d_grp", align_bytes=64)
             interleave(copy, d_grp[c], d_perm[c], ts[0] * P, ts[1] * P)
+
+        def scale_next(c):
+            scaled[c] = stage.tile([P, PACK, F], F32, name="scaled")
+            for j in range(PACK):
+                nc.scalar.activation(
+                    out=scaled[c][:, j, :].rearrange("p (t m) -> p t m", t=PACK),
+                    in_=n_raw[c // G][:, c % G, j, :].rearrange("p (m t) -> p t m", t=PACK),
+                    func=ACT.Copy,
+                    scale=neg_disc[:, j, c : c + 1],
+                )
+
+        def add_interleaved(c, t):
+            if c not in d_grp:
+                d_grp[c] = stage.tile([P, F, PACK], BF16, name="d_grp", align_bytes=64)
+            cols = slice(t * P, (t + 1) * P)
+            nc.vector.tensor_tensor(
+                out=d_grp[c][:, cols, :].rearrange("p (m i) j -> p m j i", i=4),
+                in0=p_raw[c // G][:, c % G, :, :].rearrange("p j (m i t) -> p t m j i", i=4, t=PACK)[:, t, :, :, :],
+                in1=scaled[c][:, :, cols].rearrange("p j (m i) -> p m j i", i=4),
+                op=ALU.add,
+            )
+
+        def inter_d_cols(c, first, end, copy):
+            if c not in d_grp:
+                d_grp[c] = stage.tile([P, F, PACK], BF16, name="d_grp", align_bytes=64)
+            interleave(copy, d_grp[c], d_perm[c], first, end)
 
         def quant(c, grp, cd, sc, kind, lo, hi):
             if c not in cd:
@@ -220,9 +242,9 @@ def tile_lstd_head_residuals_s14_kernel(tc, z, phi, nxt, disc, w_words, w_scales
                 )
 
         def empty_o(on_vector, h, i, s):
-            if (h, i) not in result:
-                result[h, i] = results.tile([P, N], F32, name="result")
-            dst = result[h, i][:, HALF * s : HALF * (s + 1)]
+            if (h, i // 2) not in result:
+                result[h, i // 2] = results.tile([P, 2, N], F32, name="result")
+            dst = result[h, i // 2][:, i % 2, HALF * s : HALF * (s + 1)]
             bias = b_cols[:, i, h : h + 1]
             if on_vector:
                 nc.vector.tensor_scalar(
@@ -232,17 +254,19 @@ def tile_lstd_head_residuals_s14_kernel(tc, z, phi, nxt, disc, w_words, w_scales
                 nc.scalar.activation(out=dst, in_=bank_o[h, i, s][:], func=ACT.Identity, bias=bias, scale=-1.0)
 
         def store(h, i, lo=0, hi=N):
-            nc.sync.dma_start(out=out[h, i * P : (i + 1) * P, lo:hi], in_=result[h, i][:, lo:hi])
+            nc.sync.dma_start(out=out[h, i * P : (i + 1) * P, lo:hi], in_=result[h, i // 2][:, i % 2, lo:hi])
+
+        def store_pair(h, k):
+            rows_out = out[h, 2 * P * k : 2 * P * (k + 1), :].rearrange("(i p) n -> p i n", i=2)
+            nc.sync.dma_start(out=rows_out, in_=result[h, k][:])
 
         s_copy, v_copy = nc.scalar.copy, nc.vector.tensor_copy
 
         inter_z(0)
-        inter_z(1)
-        inter_z(2)
-        inter_z(3)
         last = CHUNKS - 1
         ZPOS = 2
-        V_O = (((0,1),), ((0,1),), ())
+        V_O = ((), (), ())
+        EARLY = 0
         lo, hi = (0, PACK // 2), (PACK // 2, PACK)
         for c in range(CHUNKS):
             h = c // G - 1
@@ -257,7 +281,7 @@ def tile_lstd_head_residuals_s14_kernel(tc, z, phi, nxt, disc, w_words, w_scales
                         for i in range(TILES):
                             first_product(h, i)
                             empty_a(s_copy, h, i)
-                if q == 1 and c == 1:
+                if q == 3 and c == 1:
                     turned_b = psum_a.tile([P, TILES, P], BF16, name="bank_a")
                     for i in range(TILES):
                         nc.tensor.transpose(turned_b[:, i, :], b_rows[:, i * P : (i + 1) * P], ident[:])
@@ -266,11 +290,15 @@ def tile_lstd_head_residuals_s14_kernel(tc, z, phi, nxt, disc, w_words, w_scales
                     quant_a(h, q - 1, 2)
                     second_product(h, q - 1)
                     second_product(h, q)
+            if c < EARLY:
+                inter_d(c, hi, s_copy)
+            for k in {0: (1,), 1: (2, 3)}.get(c, ()):
+                inter_z(k)
             quant_z(c)
             if late:
                 for i, s in V_O[h]:
                     empty_o(True, h, i, s)
-            inter_d(c, parts[0])
+            inter_d(c, lo if c < EARLY else parts[0])
             if c == last:
                 diff(c, 0, hi)
                 quant_d(c, lo)
@@ -288,7 +316,8 @@ def tile_lstd_head_residuals_s14_kernel(tc, z, phi, nxt, disc, w_words, w_scales
                     for s in range(HALVES):
                         if (i, s) not in V_O[h]:
                             empty_o(False, h, i, s)
-                    store(h, i)
+                    if i % 2 == 1:
+                        store_pair(h, i // 2)
 
         h = H - 1
         quant_d(last, hi)
@@ -307,7 +336,10 @@ def tile_lstd_head_residuals_s14_kernel(tc, z, phi, nxt, disc, w_words, w_scales
         for i in range(TILES):
             for s in range(HALVES):
                 empty_o(s == 1, h, i, s)
-                store(h, i, s * HALF, (s + 1) * HALF)
+                if i in (0, TILES - 1):
+                    store(h, i, s * HALF, (s + 1) * HALF)
+            if i in (1, 2):
+                store(h, i)
             if i == 0:
                 quant_a(h, 3, 1)
                 second_product(h, 3)

from contextlib import ExitStack

import concourse.mybir as mybir
from concourse.masks import make_identity

H, T, F, N = 4, 1024, 512, 1024
FLOPS = 2 * H * F * F * T + 2 * H * F * F * N

F32 = mybir.dt.float32
BF16 = mybir.dt.bfloat16
U32 = mybir.dt.uint32
I32 = mybir.dt.int32
U8 = mybir.dt.uint8
FP8X4 = mybir.dt.float8_e4m3fn_x4
FP4X4 = mybir.dt.float4_e2m1fn_x4
ACT = mybir.ActivationFunctionType
ALU = mybir.AluOpType

P = 128
PACK = 4
K_PASS = P * PACK
G = T // K_PASS
CHUNKS = H * G
TILES = F // P
HALF = 512
HALVES = N // HALF


def tile_lstd_head_residuals_s14_kernel(tc, z, phi, nxt, disc, w_words, w_scales, b, out):
    nc = tc.nc
    with ExitStack() as ctx:
        raw = ctx.enter_context(tc.tile_pool(name="raw", bufs=H))
        stage = ctx.enter_context(tc.tile_pool(name="stage", bufs=2))
        zstage = ctx.enter_context(tc.tile_pool(name="zstage", bufs=4))
        codes = ctx.enter_context(tc.tile_pool(name="codes", bufs=4))
        acodes = ctx.enter_context(tc.tile_pool(name="acodes", bufs=4))
        results = ctx.enter_context(tc.tile_pool(name="results", bufs=4))
        keep = ctx.enter_context(tc.tile_pool(name="keep", bufs=1))
        psum_a = ctx.enter_context(tc.psum_pool(name="psum_a", bufs=4))
        psum_o = ctx.enter_context(tc.psum_pool(name="psum_o", bufs=4))
        ctx.enter_context(tc.manual_schedule())

        rows = keep.tile([P, F], BF16, name="rows")
        b_rows = keep.tile([P, F], BF16, name="b_rows")
        w_sb = keep.tile([P, H, 2 * N], U8, name="w_sb", align_bytes=64)
        ws_sb = keep.tile([P, H, N], U8, name="ws_sb", align_bytes=64)
        ident = keep.tile([P, P], BF16, name="ident")
        neg_disc = keep.tile([P, PACK, CHUNKS], F32, name="neg_disc")
        b_cols = keep.tile([P, TILES, H], F32, name="b_cols")
        warm = keep.tile([P, 2], F32, name="warm")

        nc.gpsimd.memset(rows[:].bitcast(I32), 0)
        nc.vector.memset(warm[:], 0.0)
        nc.vector.memset(b_rows[:], 0.0)
        nc.vector.memset(ws_sb[:].rearrange("p g n -> p (g n)").bitcast(I32), 0)
        make_identity(nc, ident[:])

        z_raw, n_raw, p_raw = [], [], []
        for h in range(H):
            z_head = raw.tile([P, G, PACK, F], BF16, name="z_head")
            n_head = raw.tile([P, G, PACK, F], BF16, name="n_head")
            p_head = raw.tile([P, G, PACK, F], BF16, name="p_head")
            z_raw.append(z_head)
            n_raw.append(n_head)
            p_raw.append(p_head)

        def load_rows(dst, src, c, j0=0, j1=PACK):
            h, g = divmod(c, G)
            view = src[h, g * K_PASS : (g + 1) * K_PASS, :].rearrange("(p j) w -> p j w", j=PACK)
            nc.sync.dma_start(out=dst[h][:, g, j0:j1, :], in_=view[:, j0:j1, :])

        def load_head(dst, src, h):
            nc.sync.dma_start(out=dst[h][:], in_=src[h].rearrange("(g p j) w -> p g j w", g=G, j=PACK))

        nc.scalar.activation(out=warm[:, 1:2], in_=warm[:, 0:1], func=ACT.Identity)
        load_rows(z_raw, z, 0)
        nc.sync.dma_start(out=rows[0:CHUNKS, :], in_=disc.rearrange("h (g x) -> (h g) x", g=G))
        load_rows(n_raw, nxt, 0, 0, 2)
        load_rows(p_raw, phi, 0, 0, 2)
        load_rows(n_raw, nxt, 0, 2, 4)
        load_rows(p_raw, phi, 0, 2, 4)
        load_rows(z_raw, z, 1)
        nc.sync.dma_start(out=b_rows[0:H, :], in_=b)
        load_rows(n_raw, nxt, 1)
        load_rows(p_raw, phi, 1)
        load_rows(z_raw, z, 2)
        load_rows(n_raw, nxt, 2)
        load_rows(p_raw, phi, 2)
        load_rows(z_raw, z, 3)
        for r in range(4):
            nc.sync.dma_start(
                out=ws_sb[r:P:32, :, :].bitcast(I32),
                in_=w_scales[:, r:16:4, :].rearrange("g q n -> q g n").bitcast(I32),
            )
        nc.sync.dma_start(out=w_sb[:, 0:1, :].bitcast(I32), in_=w_words[0:1].rearrange("g p x -> p g x").bitcast(I32))
        load_rows(n_raw, nxt, 3)
        load_rows(p_raw, phi, 3)
        load_rows(z_raw, z, 4)
        load_rows(n_raw, nxt, 4)
        load_rows(p_raw, phi, 4)
        load_rows(z_raw, z, 5)
        load_rows(n_raw, nxt, 5)
        load_rows(p_raw, phi, 5)
        nc.sync.dma_start(out=w_sb[:, 1:4, :].bitcast(I32), in_=w_words[1:4].rearrange("g p x -> p g x").bitcast(I32))
        load_head(z_raw, z, 3)
        load_head(n_raw, nxt, 3)
        load_head(p_raw, phi, 3)

        turned = psum_a.tile([P, PACK, P], BF16, name="bank_a")
        for j in range(PACK):
            nc.tensor.transpose(turned[:, j, :], rows[:, j : F : PACK], ident[:])
        nc.vector.tensor_scalar(
            out=neg_disc[:], in0=turned[:, :, 0:CHUNKS], scalar1=-1.0, scalar2=None, op0=ALU.mult
        )

        z_grp, d_perm, d_grp, scaled = {}, {}, {}, {}
        z_codes, z_scales, d_codes, d_scales = {}, {}, {}, {}
        bank_a, bank_o, a_grp, a_codes, a_scales, result = {}, {}, {}, {}, {}, {}

        def interleave(engine_copy, dst, src, lo, hi):
            engine_copy(
                out=dst[:, lo:hi, :].rearrange("p (c i) t -> p c t i", i=4),
                in_=src[:, :, lo:hi].rearrange("p t (c i) -> p c t i", i=4),
            )

        def new_z(c):
            z_grp[c] = zstage.tile([P, F, PACK], BF16, name="z_grp", align_bytes=64)

        def inter_z(c):
            new_z(c)
            interleave(nc.scalar.copy, z_grp[c], z_raw[c // G][:, c % G, :, :], 0, F)

        def diff(c, j, ts=(0, PACK)):
            if c not in d_perm:
                d_perm[c] = stage.tile([P, PACK, F], BF16, name="d_perm")
            t = slice(ts[0], ts[1])
            nc.vector.scalar_tensor_tensor(
                out=d_perm[c][:, j, :].rearrange("p (t m) -> p t m", t=PACK)[:, t, :],
                in0=n_raw[c // G][:, c % G, j, :].rearrange("p (m t) -> p t m", t=PACK)[:, t, :],
                scalar=neg_disc[:, j, c : c + 1],
                in1=p_raw[c // G][:, c % G, j, :].rearrange("p (m t) -> p t m", t=PACK)[:, t, :],
                op0=ALU.mult,
                op1=ALU.add,
            )

        def inter_d(c, ts=(0, PACK), copy=nc.vector.tensor_copy):
            if c not in d_grp:
                d_grp[c] = stage.tile([P, F, PACK], BF16, name="d_grp", align_bytes=64)
            interleave(copy, d_grp[c], d_perm[c], ts[0] * P, ts[1] * P)

        def scale_next(c):
            scaled[c] = stage.tile([P, PACK, F], F32, name="scaled")
            for j in range(PACK):
                nc.scalar.activation(
                    out=scaled[c][:, j, :].rearrange("p (t m) -> p t m", t=PACK),
                    in_=n_raw[c // G][:, c % G, j, :].rearrange("p (m t) -> p t m", t=PACK),
                    func=ACT.Copy,
                    scale=neg_disc[:, j, c : c + 1],
                )

        def add_interleaved(c, t):
            if c not in d_grp:
                d_grp[c] = stage.tile([P, F, PACK], BF16, name="d_grp", align_bytes=64)
            cols = slice(t * P, (t + 1) * P)
            nc.vector.tensor_tensor(
                out=d_grp[c][:, cols, :].rearrange("p (m i) j -> p m j i", i=4),
                in0=p_raw[c // G][:, c % G, :, :].rearrange("p j (m i t) -> p t m j i", i=4, t=PACK)[:, t, :, :, :],
                in1=scaled[c][:, :, cols].rearrange("p j (m i) -> p m j i", i=4),
                op=ALU.add,
            )

        def inter_d_cols(c, first, end, copy):
            if c not in d_grp:
                d_grp[c] = stage.tile([P, F, PACK], BF16, name="d_grp", align_bytes=64)
            interleave(copy, d_grp[c], d_perm[c], first, end)

        def quant(c, grp, cd, sc, kind, lo, hi):
            if c not in cd:
                cd[c] = codes.tile([P, F], U32, name=kind + "_codes", align_bytes=64)
                sc[c] = codes.tile([P, F], U8, name=kind + "_scales", align_bytes=64)
            nc.vector.quantize_mx(
                out=cd[c][:, lo:hi].bitcast(FP8X4),
                scales=sc[c][:, lo:hi],
                in_=grp[c][:, lo:hi, :].rearrange("p w t -> p (w t)"),
            )

        def quant_z(c):
            quant(c, z_grp, z_codes, z_scales, "z", 0, F)

        def quant_d(c, ts=(0, PACK)):
            quant(c, d_grp, d_codes, d_scales, "d", ts[0] * P, ts[1] * P)

        def first_product(h, i, ts=(0, PACK)):
            if (h, i) not in bank_a:
                bank_a[h, i] = psum_a.tile([P, PACK, P], F32, name="bank_a")
            bank = bank_a[h, i]
            cols = slice(i * P, (i + 1) * P)
            for t in range(ts[0], ts[1]):
                m = slice(t * P, (t + 1) * P)
                for g in range(G):
                    c = h * G + g
                    nc.tensor.matmul_mx(
                        out=bank[:, t, :],
                        lhsT=d_codes[c][:, m].bitcast(FP8X4),
                        lhsT_scale=d_scales[c][:, m],
                        rhs=z_codes[c][:, cols].bitcast(FP8X4),
                        rhs_scale=z_scales[c][:, cols],
                        start=(g == 0),
                        stop=(g == G - 1),
                    )

        def empty_a(copy, h, i):
            if i % 2 == 0:
                a_grp[h, i // 2] = acodes.tile([P, 2 * P, PACK], BF16, name="a_grp", align_bytes=64)
            n = slice(i % 2 * P, (i % 2 + 1) * P)
            copy(out=a_grp[h, i // 2][:, n, :], in_=bank_a[h, i][:].rearrange("p t n -> p n t"))

        def quant_a(h, first_tile, tiles):
            k = first_tile // 2
            if (h, k) not in a_codes:
                a_codes[h, k] = acodes.tile([P, 2 * P], U32, name="a_codes", align_bytes=64)
                a_scales[h, k] = acodes.tile([P, 2 * P], U8, name="a_scales", align_bytes=64)
            n = slice(first_tile % 2 * P, (first_tile % 2 + tiles) * P)
            nc.vector.quantize_mx(
                out=a_codes[h, k][:, n].bitcast(FP8X4),
                scales=a_scales[h, k][:, n],
                in_=a_grp[h, k][:, n, :].rearrange("p n t -> p (n t)"),
            )

        def second_product(h, i):
            for s in range(HALVES):
                bank = psum_o.tile([P, HALF], F32, name="bank_o")
                bank_o[h, i, s] = bank
                nc.tensor.matmul_mx(
                    out=bank[:],
                    lhsT=a_codes[h, i // 2][:, i % 2 * P : (i % 2 + 1) * P].bitcast(FP8X4),
                    lhsT_scale=a_scales[h, i // 2][:, i % 2 * P : (i % 2 + 1) * P],
                    rhs=w_sb[:, h, 2 * HALF * s : 2 * HALF * (s + 1)].bitcast(FP4X4),
                    rhs_scale=ws_sb[:, h, HALF * s : HALF * (s + 1)],
                    start=True,
                    stop=True,
                )

        def empty_o(on_vector, h, i, s):
            if (h, i // 2) not in result:
                result[h, i // 2] = results.tile([P, 2, N], F32, name="result")
            dst = result[h, i // 2][:, i % 2, HALF * s : HALF * (s + 1)]
            bias = b_cols[:, i, h : h + 1]
            if on_vector:
                nc.vector.tensor_scalar(
                    out=dst, in0=bank_o[h, i, s][:], scalar1=-1.0, scalar2=bias, op0=ALU.mult, op1=ALU.add
                )
            else:
                nc.scalar.activation(out=dst, in_=bank_o[h, i, s][:], func=ACT.Identity, bias=bias, scale=-1.0)

        def store(h, i, lo=0, hi=N):
            nc.sync.dma_start(out=out[h, i * P : (i + 1) * P, lo:hi], in_=result[h, i // 2][:, i % 2, lo:hi])

        def store_pair(h, k):
            rows_out = out[h, 2 * P * k : 2 * P * (k + 1), :].rearrange("(i p) n -> p i n", i=2)
            nc.sync.dma_start(out=rows_out, in_=result[h, k][:])

        s_copy, v_copy = nc.scalar.copy, nc.vector.tensor_copy

        inter_z(0)
        last = CHUNKS - 1
        ZPOS = 2
        V_O = ((), (), ())
        EARLY = 0
        lo, hi = (0, PACK // 2), (PACK // 2, PACK)
        for c in range(CHUNKS):
            h = c // G - 1
            first = c % G == 0
            parts = (lo, hi) if c == last else ((0, PACK),)
            late = (h >= 0 and not first)
            for q in range(PACK):
                diff(c, q, parts[0])
                if q == 0 and c > 0:
                    quant_d(c - 1)
                    if first and h >= 0:
                        for i in range(TILES):
                            first_product(h, i)
                            empty_a(s_copy, h, i)
                if q == 3 and c == 1:
                    turned_b = psum_a.tile([P, TILES, P], BF16, name="bank_a")
                    for i in range(TILES):
                        nc.tensor.transpose(turned_b[:, i, :], b_rows[:, i * P : (i + 1) * P], ident[:])
                    nc.vector.tensor_copy(out=b_cols[:], in_=turned_b[:, :, 0:H])
                if late and q % 2 == 1:
                    quant_a(h, q - 1, 2)
                    second_product(h, q - 1)
                    second_product(h, q)
            if c < EARLY:
                inter_d(c, hi, s_copy)
            for k in {0: (1,), 1: (2, 3)}.get(c, ()):
                inter_z(k)
            quant_z(c)
            if late:
                for i, s in V_O[h]:
                    empty_o(True, h, i, s)
            inter_d(c, lo if c < EARLY else parts[0])
            if c == last:
                diff(c, 0, hi)
                quant_d(c, lo)
                for i in range(TILES):
                    first_product(H - 1, i, lo)
                for q in (1, 2, 3):
                    diff(c, q, hi)
                inter_d(c, hi)
            if h >= 0 and first and c + 2 < CHUNKS:
                inter_z(c + 2)
            if late:
                for i in range(TILES):
                    if i == ZPOS and c + 2 < CHUNKS:
                        inter_z(c + 2)
                    for s in range(HALVES):
                        if (i, s) not in V_O[h]:
                            empty_o(False, h, i, s)
                    if i % 2 == 1:
                        store_pair(h, i // 2)

        h = H - 1
        quant_d(last, hi)
        for i in range(TILES):
            first_product(h, i, hi)
        empty_a(s_copy, h, 0)
        empty_a(s_copy, h, 1)
        empty_a(s_copy, h, 2)
        quant_a(h, 0, 1)
        second_product(h, 0)
        empty_a(v_copy, h, 3)
        quant_a(h, 1, 1)
        second_product(h, 1)
        quant_a(h, 2, 1)
        second_product(h, 2)
        for i in range(TILES):
            for s in range(HALVES):
                empty_o(s == 1, h, i, s)
                if i in (0, TILES - 1):
                    store(h, i, s * HALF, (s + 1) * HALF)
            if i in (1, 2):
                store(h, i)
            if i == 0:
                quant_a(h, 3, 1)
                second_product(h, 3)
